import numpy as np
import ml_dtypes


def mxq(x, axis, fmt="e4m3"):
    dtype, down = {"e4m3": (ml_dtypes.float8_e4m3fn, 7), "e5m2": (ml_dtypes.float8_e5m2, 14)}[fmt]
    v = np.moveaxis(np.asarray(x, np.float32).astype(ml_dtypes.bfloat16).astype(np.float64), axis, -1)
    blocks = v.reshape(v.shape[:-1] + (-1, 32))
    amax = np.abs(blocks).max(-1, keepdims=True)
    byte = np.maximum(np.where(amax > 0, np.frexp(amax)[1] - 1 + 127, 0) - down, 1)
    scale = np.exp2(byte - 127.0)
    codes = (blocks / scale).astype(np.float32).astype(dtype).astype(np.float64)
    return np.moveaxis((codes * scale).reshape(v.shape), -1, axis)


WIDE = False


def mx_kscale(k):
    if not WIDE:
        return np.ones(k)
    levels = np.array([30, -30])
    if k % 512:
        return np.exp2(np.random.permutation(np.resize(levels, k // 32))).repeat(32)
    a = np.empty((k // 512, 16))
    for p in range(k // 512):
        a[p, :8] = np.random.permutation(np.resize(levels, 8))
        for g in range(8):
            far = levels[np.abs(levels - a[p, g]) >= 10]
            a[p, g + 8] = far[np.random.randint(len(far))]
    return np.exp2(a.ravel()).repeat(32)


def f64(x):
    return np.asarray(x).astype(np.float64)


def striped(idx):
    return np.tile(np.asarray(idx).reshape(-1, 16).T, (8, 1)).astype(np.uint16)


def unstriped(offs):
    return offs[:16].T.reshape(-1).astype(np.int64)


E2M1 = np.array([0.0, 0.5, 1.0, 1.5, 2.0, 3.0, 4.0, 6.0, -0.0, -0.5, -1.0, -1.5, -2.0, -3.0, -4.0, -6.0])


def pack_weight(w, fmt):
    k, n = w.shape
    w = f64(np.asarray(w, np.float32).astype(ml_dtypes.bfloat16)).reshape(k // 32, 32, n)
    amax = np.abs(w).max(1)
    if fmt in ("e4m3", "e5m2"):
        byte = np.frexp(amax)[1] - 1 + 127 - (7 if fmt == "e4m3" else 14)
    else:
        mant, ex = np.frexp(amax / 6.0)
        byte = np.where(mant > 0.5, ex, ex - 1) + 127
    byte = np.clip(np.where(amax > 0, byte, 1), 1, 254)
    scaled = (w * np.exp2(127.0 - byte)[:, None, :]).reshape(k, n).astype(np.float32)
    by_word = np.ascontiguousarray(scaled.reshape(k // 512, 128, 4, n).transpose(0, 1, 3, 2))
    if fmt in ("e4m3", "e5m2"):
        words = by_word.astype(ml_dtypes.float8_e4m3fn if fmt == "e4m3" else ml_dtypes.float8_e5m2).view(np.uint8)
    else:
        c = by_word.astype(ml_dtypes.float4_e2m1fn).view(np.uint8) & 0xF
        words = (c[..., 0::2] | (c[..., 1::2] << 4)).reshape(k // 512, 128, 2 * n)
    return np.ascontiguousarray(words), np.ascontiguousarray(byte.astype(np.uint8).reshape(k // 512, 16, n))


def unpack_weight(words, scales, fmt):
    g, _, n = scales.shape
    words = np.ascontiguousarray(words).reshape(g, 128, n, -1)
    if fmt in ("e4m3", "e5m2"):
        vals = words.view(ml_dtypes.float8_e4m3fn if fmt == "e4m3" else ml_dtypes.float8_e5m2).astype(np.float64)
    else:
        nib = np.empty((g, 128, n, 4), np.uint8)
        nib[..., 0::2] = words & 0xF
        nib[..., 1::2] = words >> 4
        vals = E2M1[nib]
    vals = vals * np.repeat(np.exp2(scales.astype(np.float64) - 127.0), 8, axis=1)[..., None]
    return vals.transpose(0, 1, 3, 2).reshape(g * 512, n)


K, T, J, I, R, C, S = 512, 512, 256, 256, 512, 512, 32


def setup_inputs():
    n = np.random.standard_normal
    idx = np.random.permutation(T)[:J]
    idx2 = np.random.permutation(C)[:J]
    idx3 = np.random.permutation(T)[:I]
    fk = mx_kscale(K)
    fr = mx_kscale(R)
    xtp = pack_weight(n((K, T)) / fk[:, None], "e5m2")
    wap = pack_weight(n((K, R)) * 0.5 / np.sqrt(K) * fk[:, None] * fr, "e4m3")
    wbp = pack_weight(n((K, R)) * 1 / np.sqrt(K) * fk[:, None] / fr, "e2m1")
    return {
        "xt_words": xtp[0],
        "xt_scales": xtp[1],
        "wa_words": wap[0],
        "wa_scales": wap[1],
        "tf": (n((R, C))).astype(np.float32),
        "wb_words": wbp[0],
        "wb_scales": wbp[1],
        "ob": (n((R, I)) * 0.5 / fr[:, None]).astype(np.float32),
        "bi": (np.random.uniform(-15.0, 15.0, (1, I))).astype(np.float32),
        "offs": striped(idx),
        "offs2": striped(idx2),
        "offs3": striped(idx3),
    }


def reference(xt_words, xt_scales, wa_words, wa_scales, tf, wb_words, wb_scales, ob, bi, offs, offs2, offs3):
    idx = unstriped(offs)
    idx2 = unstriped(offs2)
    idx3 = unstriped(offs3)
    xtu = unpack_weight(xt_words, xt_scales, "e5m2")
    wau = unpack_weight(wa_words, wa_scales, "e4m3")
    wbu = unpack_weight(wb_words, wb_scales, "e2m1")
    xtidxg = xtu[:, idx]
    za = wau.T @ xtidxg
    ha = za * f64(tf)[:, idx2]
    xtidx3g = xtu[:, idx3]
    zb = wbu.T @ xtidx3g
    hb = np.maximum(zb, f64(ob))
    haq = mxq(ha, 0, "e5m2")
    hbq = mxq(hb, 0, "e4m3")
    a0 = haq.T @ hbq
    a = a0 + f64(bi)
    g1 = a.reshape(J, S, I // S).max(axis=2)
    y = 0.04 * g1
    return y

@@ -1,0 +1,196 @@
+from contextlib import ExitStack
+
+import concourse.mybir as mybir
+from concourse.masks import make_identity
+
+F32 = mybir.dt.float32
+BF16 = mybir.dt.bfloat16
+I32 = mybir.dt.int32
+U32 = mybir.dt.uint32
+U16 = mybir.dt.uint16
+U8 = mybir.dt.uint8
+E4M3 = mybir.dt.float8_e4m3fn_x4
+E5M2 = mybir.dt.float8_e5m2_x4
+E2M1 = mybir.dt.float4_e2m1fn_x4
+ALU = mybir.AluOpType
+COPY = mybir.ActivationFunctionType.Copy
+
+P = 128
+K, T, J, I, R, C, S = 512, 512, 256, 256, 512, 512, 32
+PACK = 4
+HALF = 128
+OUT_SCALE = 0.04
+FLOPS = 2 * K * R * J + 2 * K * R * I + 2 * R * J * I
+
+
+def tile_list_meet_timestable_added_bundlemax_kernel(
+    tc, xt_words, xt_scales, wa_words, wa_scales, tf, wb_words, wb_scales, ob, bi, offs, offs2, offs3, out
+):
+    nc = tc.nc
+    with ExitStack() as ctx:
+        sb = ctx.enter_context(tc.tile_pool(name="sb", bufs=1))
+        ps = ctx.enter_context(tc.psum_pool(name="ps", bufs=1))
+
+        def tile(shape, dtype, name):
+            return sb.tile(shape, dtype, name=name, align_bytes=64)
+
+        def load_scales(queue, plane, rows, quadrants):
+            src = rows[0].bitcast(I32)
+            for q in quadrants:
+                queue.dma_start(
+                    out=plane[32 * q : 32 * q + 32, :].bitcast(I32),
+                    in_=src[4 * q : 4 * q + 4, :].unsqueeze(0).to_broadcast([8, 4, R // 4]),
+                )
+
+        list_a = tile([P, J // 16], U16, "list_a")
+        list_f = tile([P, J // 16], U16, "list_f")
+        list_b = tile([P, I // 16], U16, "list_b")
+        xt_w = tile([P, T], I32, "xt_w")
+        xt_s = tile([P, T], U8, "xt_s")
+        wa_w = tile([P, R], I32, "wa_w")
+        wa_s = tile([P, R], U8, "wa_s")
+        wb_w = tile([P, 2 * R], U8, "wb_w")
+        wb_s = tile([P, R], U8, "wb_s")
+        tf_part0 = tile([P, 3, C], F32, "tf_part0")
+        tf_part1 = tile([P, 1, C], F32, "tf_part1")
+        tf_rows = [tf_part0[:, 0, :], tf_part0[:, 1, :], tf_part0[:, 2, :], tf_part1[:, 0, :]]
+        ob_rows = tile([P, PACK, I], F32, "ob_rows")
+        bi_pairs = tile([P, 2], F32, "bi_pairs")
+        ident = tile([P, P], F32, "ident")
+
+        tf_dealt = tf.rearrange("(p t) c -> p t c", t=PACK)
+        ob_dealt = ob.rearrange("(p t) i -> p t i", t=PACK)
+
+        nc.sync.dma_start(list_b[:], offs3)
+        load_scales(nc.scalar, xt_s, xt_scales, range(4))
+        nc.sync.dma_start(list_a[:], offs)
+        nc.sync.dma_start(out=xt_w[:], in_=xt_words[0].rearrange("p c r -> p (c r)").bitcast(I32))
+        nc.sync.dma_start(out=tf_part0[:], in_=tf_dealt[:, 0:3, :])
+        make_identity(nc, ident[:])
+        nc.sync.dma_start(out=wb_w[:].bitcast(I32), in_=wb_words[0].bitcast(I32))
+        load_scales(nc.sync, wb_s, wb_scales, range(4))
+        nc.sync.dma_start(list_f[:], offs2)
+        nc.sync.dma_start(out=ob_rows[:], in_=ob_dealt)
+        nc.sync.dma_start(out=wa_w[:], in_=wa_words[0].rearrange("p c r -> p (c r)").bitcast(I32))
+        load_scales(nc.sync, wa_s, wa_scales, range(4))
+        nc.sync.dma_start(out=tf_part1[:], in_=tf_dealt[:, 3:4, :])
+        nc.sync.dma_start(out=bi_pairs[:], in_=bi.rearrange("o (p m) -> p (o m)", m=2))
+
+        xa_w = tile([P, J], U32, "xa_w")
+        xa_s = tile([P, J], U8, "xa_s")
+        xb_w = tile([P, I], U32, "xb_w")
+        xb_s = tile([P, I], U8, "xb_s")
+
+        def deal(copy, dst, src, run):
+            copy(
+                out=dst.rearrange("p (t c i) -> p c t i", t=PACK, i=run),
+                in_=src.rearrange("p (c i t) -> p c t i", t=PACK, i=run),
+            )
+
+        wa_wd = tile([P, R], U32, "wa_wd")
+        wa_sd = tile([P, R], U8, "wa_sd")
+        wb_wd = tile([P, 2 * R], U8, "wb_wd")
+        wb_sd = tile([P, R], U8, "wb_sd")
+        tf_picked = tile([P, PACK, J], F32, "tf_picked")
+
+        def pick_tf(t):
+            nc.scalar.activation(out=tf_picked[:, t, :], in_=tf_rows[t].indirect(list_f[:]), func=COPY)
+
+        def pick_words(dst, picks):
+            nc.vector.tensor_copy(out=dst[:], in_=xt_w[:].bitcast(U32).indirect(picks[:]))
+
+        def pick_scales(dst, picks):
+            nc.vector.tensor_copy(out=dst[:], in_=xt_s[:].indirect(picks[:]))
+
+        pick_scales(xb_s, list_b)
+        pick_words(xb_w, list_b)
+        pick_scales(xa_s, list_a)
+        deal(nc.vector.tensor_copy, wb_wd[:].bitcast(U16), wb_w[:].bitcast(U16), 8)
+        deal(nc.vector.tensor_copy, wb_sd[:], wb_s[:], 16)
+        pick_words(xa_w, list_a)
+        for t in range(3):
+            pick_tf(t)
+        deal(nc.vector.tensor_copy, wa_wd[:], wa_w[:].bitcast(U32), 4)
+        deal(nc.vector.tensor_copy, wa_sd[:], wa_s[:], 16)
+        nc.vector.tensor_copy(out=tf_picked[:, 3, :HALF], in_=tf_rows[3].indirect(list_f[:, : HALF // 16]))
+        nc.scalar.activation(out=tf_picked[:, 3, HALF:], in_=tf_rows[3].indirect(list_f[:, HALF // 16 :]), func=COPY)
+
+        bi_ps = ps.tile([P, 2, P], F32, name="bi_ps")
+        for m in range(2):
+            nc.tensor.transpose(bi_ps[:, m, :], bi_pairs[:, m : m + 1].to_broadcast([P, P]), ident[:])
+        bias = tile([P, I], F32, "bias")
+        nc.scalar.activation(
+            out=bias[:].rearrange("p (n m) -> p n m", m=2),
+            in_=bi_ps[:].rearrange("p m n -> p n m"),
+            func=COPY,
+            scale=OUT_SCALE,
+        )
+
+        def first_stage(name, weights, weight_scales, x_w, x_s, h):
+            z = ps.tile([P, PACK, HALF], F32, name=name)
+            cols = slice(h * HALF, (h + 1) * HALF)
+            for t in range(PACK):
+                nc.tensor.matmul_mx(
+                    out=z[:, t, :],
+                    lhsT=weights(t),
+                    lhsT_scale=weight_scales[:, t * P : (t + 1) * P],
+                    rhs=x_w[:, cols].bitcast(E5M2),
+                    rhs_scale=x_s[:, cols],
+                    start=True,
+                    stop=True,
+                )
+            return z
+
+        def combine(woven, z, other, op):
+            nc.vector.tensor_tensor(
+                out=woven.rearrange("p (c i t) -> p c t i", t=PACK, i=4),
+                in0=z[:].rearrange("p t (c i) -> p c t i", i=4),
+                in1=other.rearrange("p t (c i) -> p c t i", i=4),
+                op=op,
+            )
+
+        def quantise(name, woven, width, fmt):
+            words = tile([P, width], U32, name + "_w")
+            scales = tile([P, width], U8, name + "_s")
+            nc.vector.quantize_mx(out=words[:].bitcast(fmt), scales=scales[:], in_=woven)
+            return words, scales
+
+        zb = [
+            first_stage("zb%d" % h, lambda t: wb_wd[:, 2 * t * P : 2 * (t + 1) * P].bitcast(E2M1), wb_sd, xb_w, xb_s, h)
+            for h in range(2)
+        ]
+        hb = tile([P, I * PACK], BF16, "hb")
+        for h in range(2):
+            combine(hb[:, h * HALF * PACK : (h + 1) * HALF * PACK], zb[h], ob_rows[:, :, h * HALF : (h + 1) * HALF], ALU.max)
+        hb_w, hb_s = quantise("hbq", hb[:], I, E4M3)
+
+        za = [
+            first_stage("za%d" % h, lambda t: wa_wd[:, t * P : (t + 1) * P].bitcast(E4M3), wa_sd, xa_w, xa_s, h)
+            for h in range(2)
+        ]
+        best = tile([P, 2, S], F32, "best")
+        for h in range(2):
+            ha = tile([P, HALF * PACK], BF16, "ha%d" % h)
+            combine(ha[:], za[h], tf_picked[:, :, h * HALF : (h + 1) * HALF], ALU.mult)
+            ha_w, ha_s = quantise("haq%d" % h, ha[:], HALF, E5M2)
+            acc = ps.tile([P, I], F32, name="acc%d" % h)
+            nc.tensor.matmul_mx(
+                out=acc[:],
+                lhsT=ha_w[:].bitcast(E5M2),
+                lhsT_scale=ha_s[:],
+                rhs=hb_w[:].bitcast(E4M3),
+                rhs_scale=hb_s[:],
+                start=True,
+                stop=True,
+            )
+            scores = tile([P, I], F32, "scores%d" % h)
+            nc.vector.scalar_tensor_tensor(
+                out=scores[:], in0=acc[:], scalar=OUT_SCALE, in1=bias[:], op0=ALU.mult, op1=ALU.add
+            )
+            nc.vector.tensor_reduce(
+                out=best[:, h, :],
+                in_=scores[:].rearrange("p (s e) -> p s e", e=I // S),
+                axis=mybir.AxisListType.X,
+                op=ALU.max,
+            )
+        nc.sync.dma_start(out=out.rearrange("(j p) s -> p j s", p=P), in_=best[:])

@@ -51,30 +51,35 @@ def tile_list_meet_timestable_added_bundlemax_kernel(
         wa_s = tile([P, R], U8, "wa_s")
         wb_w = tile([P, 2 * R], U8, "wb_w")
         wb_s = tile([P, R], U8, "wb_s")
-        tf_part0 = tile([P, 3, C], F32, "tf_part0")
+        tf_part0 = tile([P, 2, C], F32, "tf_part0")
         tf_part1 = tile([P, 1, C], F32, "tf_part1")
-        tf_rows = [tf_part0[:, 0, :], tf_part0[:, 1, :], tf_part0[:, 2, :], tf_part1[:, 0, :]]
-        ob_rows = tile([P, PACK, I], F32, "ob_rows")
+        tf_part2 = tile([P, 1, C], F32, "tf_part2")
+        tf_rows = [tf_part0[:, 0, :], tf_part0[:, 1, :], tf_part1[:, 0, :], tf_part2[:, 0, :]]
+        shared = tile([P, 640 + PACK * I], F32, "shared")
+        ob_rows = shared[:, 640:].rearrange("p (t i) -> p t i", t=PACK)
+        tf_picked = shared[:, : PACK * J].rearrange("p (t j) -> p t j", t=PACK)
         bi_pairs = tile([P, 2], F32, "bi_pairs")
         ident = tile([P, P], F32, "ident")
 
         tf_dealt = tf.rearrange("(p t) c -> p t c", t=PACK)
         ob_dealt = ob.rearrange("(p t) i -> p t i", t=PACK)
 
-        nc.sync.dma_start(list_b[:], offs3)
-        load_scales(nc.scalar, xt_s, xt_scales, range(4))
-        nc.sync.dma_start(list_a[:], offs)
-        nc.sync.dma_start(out=xt_w[:], in_=xt_words[0].rearrange("p c r -> p (c r)").bitcast(I32))
-        nc.sync.dma_start(out=tf_part0[:], in_=tf_dealt[:, 0:3, :])
+        nc.gpsimd.dma_start(out=bi_pairs[:], in_=bi.rearrange("o (p m) -> p (o m)", m=2))
         make_identity(nc, ident[:])
+        nc.sync.dma_start(list_b[:], offs3)
+        load_scales(nc.scalar, xt_s, xt_scales, range(3))
+        load_scales(nc.sync, xt_s, xt_scales, [3])
+        nc.sync.dma_start(out=xt_w[:], in_=xt_words[0].rearrange("p c r -> p (c r)").bitcast(I32))
+        nc.sync.dma_start(list_f[:], offs2)
+        nc.sync.dma_start(out=tf_part0[:], in_=tf_dealt[:, 0:2, :])
         nc.sync.dma_start(out=wb_w[:].bitcast(I32), in_=wb_words[0].bitcast(I32))
         load_scales(nc.sync, wb_s, wb_scales, range(4))
-        nc.sync.dma_start(list_f[:], offs2)
-        nc.sync.dma_start(out=ob_rows[:], in_=ob_dealt)
+        nc.sync.dma_start(list_a[:], offs)
+        nc.sync.dma_start(out=ob_rows, in_=ob_dealt)
         nc.sync.dma_start(out=wa_w[:], in_=wa_words[0].rearrange("p c r -> p (c r)").bitcast(I32))
         load_scales(nc.sync, wa_s, wa_scales, range(4))
-        nc.sync.dma_start(out=tf_part1[:], in_=tf_dealt[:, 3:4, :])
-        nc.sync.dma_start(out=bi_pairs[:], in_=bi.rearrange("o (p m) -> p (o m)", m=2))
+        nc.sync.dma_start(out=tf_part1[:], in_=tf_dealt[:, 2:3, :])
+        nc.sync.dma_start(out=tf_part2[:], in_=tf_dealt[:, 3:4, :])
 
         xa_w = tile([P, J], U32, "xa_w")
         xa_s = tile([P, J], U8, "xa_s")
@@ -91,10 +96,13 @@ def tile_list_meet_timestable_added_bundlemax_kernel(
         wa_sd = tile([P, R], U8, "wa_sd")
         wb_wd = tile([P, 2 * R], U8, "wb_wd")
         wb_sd = tile([P, R], U8, "wb_sd")
-        tf_picked = tile([P, PACK, J], F32, "tf_picked")
 
-        def pick_tf(t):
-            nc.scalar.activation(out=tf_picked[:, t, :], in_=tf_rows[t].indirect(list_f[:]), func=COPY)
+        def pick_tf(t, first, last, on_vector):
+            window = tf_rows[t].indirect(list_f[:, first // 16 : last // 16])
+            if on_vector:
+                nc.vector.tensor_copy(out=tf_picked[:, t, first:last], in_=window)
+            else:
+                nc.scalar.activation(out=tf_picked[:, t, first:last], in_=window, func=COPY)
 
         def pick_words(dst, picks):
             nc.vector.tensor_copy(out=dst[:], in_=xt_w[:].bitcast(U32).indirect(picks[:]))
@@ -104,16 +112,15 @@ def tile_list_meet_timestable_added_bundlemax_kernel(
 
         pick_scales(xb_s, list_b)
         pick_words(xb_w, list_b)
-        pick_scales(xa_s, list_a)
         deal(nc.vector.tensor_copy, wb_wd[:].bitcast(U16), wb_w[:].bitcast(U16), 8)
         deal(nc.vector.tensor_copy, wb_sd[:], wb_s[:], 16)
+        pick_scales(xa_s, list_a)
         pick_words(xa_w, list_a)
-        for t in range(3):
-            pick_tf(t)
-        deal(nc.vector.tensor_copy, wa_wd[:], wa_w[:].bitcast(U32), 4)
-        deal(nc.vector.tensor_copy, wa_sd[:], wa_s[:], 16)
-        nc.vector.tensor_copy(out=tf_picked[:, 3, :HALF], in_=tf_rows[3].indirect(list_f[:, : HALF // 16]))
-        nc.scalar.activation(out=tf_picked[:, 3, HALF:], in_=tf_rows[3].indirect(list_f[:, HALF // 16 :]), func=COPY)
+        pick_tf(0, 0, J, False)
+        pick_tf(1, 0, J, False)
+        deal(nc.scalar.copy, wa_wd[:], wa_w[:].bitcast(U32), 4)
+        deal(nc.gpsimd.tensor_copy, wa_sd[:], wa_s[:], 16)
+        pick_tf(2, 0, HALF, False)
 
         bi_ps = ps.tile([P, 2, P], F32, name="bi_ps")
         for m in range(2):
@@ -162,6 +169,9 @@ def tile_list_meet_timestable_added_bundlemax_kernel(
         hb = tile([P, I * PACK], BF16, "hb")
         for h in range(2):
             combine(hb[:, h * HALF * PACK : (h + 1) * HALF * PACK], zb[h], ob_rows[:, :, h * HALF : (h + 1) * HALF], ALU.max)
+        pick_tf(3, 0, HALF, True)
+        pick_tf(2, HALF, J, False)
+        pick_tf(3, HALF, J, False)
         hb_w, hb_s = quantise("hbq", hb[:], I, E4M3)
 
         za = [

@@ -31,8 +31,8 @@ def tile_list_meet_timestable_added_bundlemax_kernel(
         sb = ctx.enter_context(tc.tile_pool(name="sb", bufs=1))
         ps = ctx.enter_context(tc.psum_pool(name="ps", bufs=1))
 
-        def tile(shape, dtype, name):
-            return sb.tile(shape, dtype, name=name, align_bytes=64)
+        def tile(shape, dtype, name, tag=None):
+            return sb.tile(shape, dtype, name=name, tag=tag or name, align_bytes=64)
 
         def load_scales(queue, plane, rows, quadrants):
             src = rows[0].bitcast(I32)
@@ -55,33 +55,31 @@ def tile_list_meet_timestable_added_bundlemax_kernel(
         tf_part1 = tile([P, 1, C], F32, "tf_part1")
         tf_part2 = tile([P, 1, C], F32, "tf_part2")
         tf_rows = [tf_part0[:, 0, :], tf_part0[:, 1, :], tf_part1[:, 0, :], tf_part2[:, 0, :]]
-        shared = tile([P, 640 + PACK * I], F32, "shared")
-        ob_rows = shared[:, 640:].rearrange("p (t i) -> p t i", t=PACK)
-        tf_picked = shared[:, : PACK * J].rearrange("p (t j) -> p t j", t=PACK)
+        ob_rows = tile([P, PACK, I], F32, "ob_rows")
+        tf_picked = tile([P, PACK, J], F32, "tf_picked")
         bi_pairs = tile([P, 2], F32, "bi_pairs")
         ident = tile([P, P], F32, "ident")
 
         tf_dealt = tf.rearrange("(p t) c -> p t c", t=PACK)
         ob_dealt = ob.rearrange("(p t) i -> p t i", t=PACK)
 
+        nc.gpsimd.dma_start(out=wb_w[:].bitcast(I32), in_=wb_words[0].bitcast(I32))
+        nc.gpsimd.dma_start(out=wa_w[:], in_=wa_words[0].rearrange("p c r -> p (c r)").bitcast(I32))
         nc.gpsimd.dma_start(out=bi_pairs[:], in_=bi.rearrange("o (p m) -> p (o m)", m=2))
         make_identity(nc, ident[:])
         nc.sync.dma_start(list_b[:], offs3)
         load_scales(nc.scalar, xt_s, xt_scales, range(3))
         load_scales(nc.sync, xt_s, xt_scales, [3])
         nc.sync.dma_start(out=xt_w[:], in_=xt_words[0].rearrange("p c r -> p (c r)").bitcast(I32))
-        nc.sync.dma_start(list_f[:], offs2)
-        nc.sync.dma_start(out=tf_part0[:], in_=tf_dealt[:, 0:2, :])
-        nc.sync.dma_start(out=wb_w[:].bitcast(I32), in_=wb_words[0].bitcast(I32))
-        load_scales(nc.sync, wb_s, wb_scales, range(4))
         nc.sync.dma_start(list_a[:], offs)
-        nc.sync.dma_start(out=ob_rows, in_=ob_dealt)
-        nc.sync.dma_start(out=wa_w[:], in_=wa_words[0].rearrange("p c r -> p (c r)").bitcast(I32))
+        nc.sync.dma_start(out=tf_part0[:], in_=tf_dealt[:, 0:2, :])
+        load_scales(nc.sync, wb_s, wb_scales, range(4))
+        nc.sync.dma_start(list_f[:], offs2)
+        nc.sync.dma_start(out=ob_rows[:], in_=ob_dealt)
         load_scales(nc.sync, wa_s, wa_scales, range(4))
         nc.sync.dma_start(out=tf_part1[:], in_=tf_dealt[:, 2:3, :])
         nc.sync.dma_start(out=tf_part2[:], in_=tf_dealt[:, 3:4, :])
 
-        xa_w = tile([P, J], U32, "xa_w")
         xa_s = tile([P, J], U8, "xa_s")
         xb_w = tile([P, I], U32, "xb_w")
         xb_s = tile([P, I], U8, "xb_s")
@@ -97,12 +95,9 @@ def tile_list_meet_timestable_added_bundlemax_kernel(
         wb_wd = tile([P, 2 * R], U8, "wb_wd")
         wb_sd = tile([P, R], U8, "wb_sd")
 
-        def pick_tf(t, first, last, on_vector):
+        def pick_tf(t, first, last):
             window = tf_rows[t].indirect(list_f[:, first // 16 : last // 16])
-            if on_vector:
-                nc.vector.tensor_copy(out=tf_picked[:, t, first:last], in_=window)
-            else:
-                nc.scalar.activation(out=tf_picked[:, t, first:last], in_=window, func=COPY)
+            nc.scalar.activation(out=tf_picked[:, t, first:last], in_=window, func=COPY)
 
         def pick_words(dst, picks):
             nc.vector.tensor_copy(out=dst[:], in_=xt_w[:].bitcast(U32).indirect(picks[:]))
@@ -112,15 +107,17 @@ def tile_list_meet_timestable_added_bundlemax_kernel(
 
         pick_scales(xb_s, list_b)
         pick_words(xb_w, list_b)
-        deal(nc.vector.tensor_copy, wb_wd[:].bitcast(U16), wb_w[:].bitcast(U16), 8)
-        deal(nc.vector.tensor_copy, wb_sd[:], wb_s[:], 16)
         pick_scales(xa_s, list_a)
-        pick_words(xa_w, list_a)
-        pick_tf(0, 0, J, False)
-        pick_tf(1, 0, J, False)
+        deal(nc.scalar.copy, wb_wd[:].bitcast(U16), wb_w[:].bitcast(U16), 8)
         deal(nc.scalar.copy, wa_wd[:], wa_w[:].bitcast(U32), 4)
+        deal(nc.vector.tensor_copy, wb_sd[:], wb_s[:], 16)
+        xa_w = tile([P, J], U32, "xa_w", tag="wb_s")
+        pick_words(xa_w, list_a)
+        for t in range(3):
+            pick_tf(t, 0, J)
         deal(nc.gpsimd.tensor_copy, wa_sd[:], wa_s[:], 16)
-        pick_tf(2, 0, HALF, False)
+        pick_tf(3, 0, HALF)
+        pick_tf(3, HALF, J)
 
         bi_ps = ps.tile([P, 2, P], F32, name="bi_ps")
         for m in range(2):
@@ -150,9 +147,9 @@ def tile_list_meet_timestable_added_bundlemax_kernel(
 
         def combine(woven, z, other, op):
             nc.vector.tensor_tensor(
-                out=woven.rearrange("p (c i t) -> p c t i", t=PACK, i=4),
-                in0=z[:].rearrange("p t (c i) -> p c t i", i=4),
-                in1=other.rearrange("p t (c i) -> p c t i", i=4),
+                out=woven.rearrange("p (c i t) -> p c t i", t=PACK, i=2),
+                in0=z[:].rearrange("p t (c i) -> p c t i", i=2),
+                in1=other.rearrange("p t (c i) -> p c t i", i=2),
                 op=op,
             )
 
@@ -169,9 +166,6 @@ def tile_list_meet_timestable_added_bundlemax_kernel(
         hb = tile([P, I * PACK], BF16, "hb")
         for h in range(2):
             combine(hb[:, h * HALF * PACK : (h + 1) * HALF * PACK], zb[h], ob_rows[:, :, h * HALF : (h + 1) * HALF], ALU.max)
-        pick_tf(3, 0, HALF, True)
-        pick_tf(2, HALF, J, False)
-        pick_tf(3, HALF, J, False)
         hb_w, hb_s = quantise("hbq", hb[:], I, E4M3)
 
         za = [

@@ -42,6 +42,12 @@ def tile_list_meet_timestable_added_bundlemax_kernel(
                     in_=src[4 * q : 4 * q + 4, :].unsqueeze(0).to_broadcast([8, 4, R // 4]),
                 )
 
+        def load_live_rows(plane, rows):
+            nc.vector.memset(plane[:].bitcast(I32), 0)
+            src = rows[0].bitcast(I32)
+            for q in range(4):
+                nc.sync.dma_start(out=plane[32 * q : 32 * q + 4, :].bitcast(I32), in_=src[4 * q : 4 * q + 4, :])
+
         list_a = tile([P, J // 16], U16, "list_a")
         list_f = tile([P, J // 16], U16, "list_f")
         list_b = tile([P, I // 16], U16, "list_b")
@@ -65,20 +71,20 @@ def tile_list_meet_timestable_added_bundlemax_kernel(
 
         nc.gpsimd.dma_start(out=wb_w[:].bitcast(I32), in_=wb_words[0].bitcast(I32))
         nc.gpsimd.dma_start(out=wa_w[:], in_=wa_words[0].rearrange("p c r -> p (c r)").bitcast(I32))
-        nc.gpsimd.dma_start(out=bi_pairs[:], in_=bi.rearrange("o (p m) -> p (o m)", m=2))
         make_identity(nc, ident[:])
         nc.sync.dma_start(list_b[:], offs3)
         load_scales(nc.scalar, xt_s, xt_scales, range(3))
         load_scales(nc.sync, xt_s, xt_scales, [3])
-        nc.sync.dma_start(out=xt_w[:], in_=xt_words[0].rearrange("p c r -> p (c r)").bitcast(I32))
         nc.sync.dma_start(list_a[:], offs)
+        nc.sync.dma_start(out=xt_w[:], in_=xt_words[0].rearrange("p c r -> p (c r)").bitcast(I32))
         nc.sync.dma_start(out=tf_part0[:], in_=tf_dealt[:, 0:2, :])
-        load_scales(nc.sync, wb_s, wb_scales, range(4))
+        load_live_rows(wb_s, wb_scales)
         nc.sync.dma_start(list_f[:], offs2)
         nc.sync.dma_start(out=ob_rows[:], in_=ob_dealt)
-        load_scales(nc.sync, wa_s, wa_scales, range(4))
+        load_live_rows(wa_s, wa_scales)
         nc.sync.dma_start(out=tf_part1[:], in_=tf_dealt[:, 2:3, :])
         nc.sync.dma_start(out=tf_part2[:], in_=tf_dealt[:, 3:4, :])
+        nc.sync.dma_start(out=bi_pairs[:], in_=bi.rearrange("o (p m) -> p (o m)", m=2))
 
         xa_s = tile([P, J], U8, "xa_s")
         xb_w = tile([P, I], U32, "xb_w")
@@ -90,7 +96,12 @@ def tile_list_meet_timestable_added_bundlemax_kernel(
                 in_=src.rearrange("p (c i t) -> p c t i", t=PACK, i=run),
             )
 
-        wa_wd = tile([P, R], U32, "wa_wd")
+        def deal_part(copy, dst, src, run, t0, t1):
+            copy(
+                out=dst.rearrange("p (t c i) -> p c t i", t=PACK, i=run)[:, :, t0:t1, :],
+                in_=src.rearrange("p (c i t) -> p c t i", t=PACK, i=run)[:, :, t0:t1, :],
+            )
+
         wa_sd = tile([P, R], U8, "wa_sd")
         wb_wd = tile([P, 2 * R], U8, "wb_wd")
         wb_sd = tile([P, R], U8, "wb_sd")
@@ -106,13 +117,14 @@ def tile_list_meet_timestable_added_bundlemax_kernel(
             nc.vector.tensor_copy(out=dst[:], in_=xt_s[:].indirect(picks[:]))
 
         pick_scales(xb_s, list_b)
-        pick_words(xb_w, list_b)
         pick_scales(xa_s, list_a)
-        deal(nc.scalar.copy, wb_wd[:].bitcast(U16), wb_w[:].bitcast(U16), 8)
-        deal(nc.scalar.copy, wa_wd[:], wa_w[:].bitcast(U32), 4)
-        deal(nc.vector.tensor_copy, wb_sd[:], wb_s[:], 16)
-        xa_w = tile([P, J], U32, "xa_w", tag="wb_s")
+        pick_words(xb_w, list_b)
+        xa_w = tile([P, J], U32, "xa_w")
         pick_words(xa_w, list_a)
+        deal(nc.scalar.copy, wb_wd[:].bitcast(U16), wb_w[:].bitcast(U16), 8)
+        deal(nc.vector.tensor_copy, wb_sd[:], wb_s[:], 16)
+        wa_wd = tile([P, R], U32, "wa_wd", tag="wb_s")
+        deal(nc.vector.tensor_copy, wa_wd[:], wa_w[:].bitcast(U32), 4)
         for t in range(3):
             pick_tf(t, 0, J)
         deal(nc.gpsimd.tensor_copy, wa_sd[:], wa_s[:], 16)
@@ -166,7 +178,13 @@ def tile_list_meet_timestable_added_bundlemax_kernel(
         hb = tile([P, I * PACK], BF16, "hb")
         for h in range(2):
             combine(hb[:, h * HALF * PACK : (h + 1) * HALF * PACK], zb[h], ob_rows[:, :, h * HALF : (h + 1) * HALF], ALU.max)
-        hb_w, hb_s = quantise("hbq", hb[:], I, E4M3)
+        hb_w = tile([P, I], U32, "hb_w")
+        hb_s = tile([P, I], U8, "hb_s")
+        for h in range(2):
+            cols = slice(h * HALF, (h + 1) * HALF)
+            nc.vector.quantize_mx(
+                out=hb_w[:, cols].bitcast(E4M3), scales=hb_s[:, cols], in_=hb[:, h * HALF * PACK : (h + 1) * HALF * PACK]
+            )
 
         za = [
             first_stage("za%d" % h, lambda t: wa_wd[:, t * P : (t + 1) * P].bitcast(E4M3), wa_sd, xa_w, xa_s, h)

@@ -15,10 +15,13 @@ E2M1 = mybir.dt.float4_e2m1fn_x4
 ALU = mybir.AluOpType
 COPY = mybir.ActivationFunctionType.Copy
 
-P = 128
 K, T, J, I, R, C, S = 512, 512, 256, 256, 512, 512, 32
+P = 128
 PACK = 4
 HALF = 128
+GROUP = 16
+QUADRANT = 32
+LINE = 16
 OUT_SCALE = 0.04
 FLOPS = 2 * K * R * J + 2 * K * R * I + 2 * R * J * I
 
@@ -34,80 +37,76 @@ def tile_list_meet_timestable_added_bundlemax_kernel(
         def tile(shape, dtype, name, tag=None):
             return sb.tile(shape, dtype, name=name, tag=tag or name, align_bytes=64)
 
-        def load_scales(queue, plane, rows, quadrants):
+        def load_scales_repeated(queue, dst, rows, quadrants):
             src = rows[0].bitcast(I32)
             for q in quadrants:
                 queue.dma_start(
-                    out=plane[32 * q : 32 * q + 32, :].bitcast(I32),
-                    in_=src[4 * q : 4 * q + 4, :].unsqueeze(0).to_broadcast([8, 4, R // 4]),
+                    out=dst[QUADRANT * q : QUADRANT * (q + 1), :].bitcast(I32),
+                    in_=src[4 * q : 4 * q + 4, :].unsqueeze(0).to_broadcast([QUADRANT // 4, 4, T // 4]),
                 )
 
-        def load_live_rows(plane, rows):
-            nc.vector.memset(plane[:].bitcast(I32), 0)
+        def load_scales_over_zeros(dst, rows):
+            nc.vector.memset(dst[:].bitcast(I32), 0)
             src = rows[0].bitcast(I32)
             for q in range(4):
-                nc.sync.dma_start(out=plane[32 * q : 32 * q + 4, :].bitcast(I32), in_=src[4 * q : 4 * q + 4, :])
+                nc.sync.dma_start(
+                    out=dst[QUADRANT * q : QUADRANT * q + 4, :].bitcast(I32), in_=src[4 * q : 4 * q + 4, :]
+                )
 
-        list_a = tile([P, J // 16], U16, "list_a")
-        list_f = tile([P, J // 16], U16, "list_f")
-        list_b = tile([P, I // 16], U16, "list_b")
+        list_a = tile([P, J // GROUP], U16, "list_a")
+        list_f = tile([P, J // GROUP], U16, "list_f")
+        list_b = tile([P, I // GROUP], U16, "list_b")
         xt_w = tile([P, T], I32, "xt_w")
         xt_s = tile([P, T], U8, "xt_s")
         wa_w = tile([P, R], I32, "wa_w")
         wa_s = tile([P, R], U8, "wa_s")
         wb_w = tile([P, 2 * R], U8, "wb_w")
         wb_s = tile([P, R], U8, "wb_s")
-        tf_part0 = tile([P, 2, C], F32, "tf_part0")
-        tf_part1 = tile([P, 1, C], F32, "tf_part1")
-        tf_part2 = tile([P, 1, C], F32, "tf_part2")
-        tf_rows = [tf_part0[:, 0, :], tf_part0[:, 1, :], tf_part1[:, 0, :], tf_part2[:, 0, :]]
+        tf_01 = tile([P, 2, C], F32, "tf_01")
+        tf_2 = tile([P, 1, C], F32, "tf_2")
+        tf_3 = tile([P, 1, C], F32, "tf_3")
+        tf_rows = [tf_01[:, 0, :], tf_01[:, 1, :], tf_2[:, 0, :], tf_3[:, 0, :]]
         ob_rows = tile([P, PACK, I], F32, "ob_rows")
         tf_picked = tile([P, PACK, J], F32, "tf_picked")
         bi_pairs = tile([P, 2], F32, "bi_pairs")
         ident = tile([P, P], F32, "ident")
 
-        tf_dealt = tf.rearrange("(p t) c -> p t c", t=PACK)
-        ob_dealt = ob.rearrange("(p t) i -> p t i", t=PACK)
+        tf_by_t = tf.rearrange("(p t) c -> p t c", t=PACK)
+        ob_by_t = ob.rearrange("(p t) i -> p t i", t=PACK)
 
         nc.gpsimd.dma_start(out=wb_w[:].bitcast(I32), in_=wb_words[0].bitcast(I32))
         nc.gpsimd.dma_start(out=wa_w[:], in_=wa_words[0].rearrange("p c r -> p (c r)").bitcast(I32))
         make_identity(nc, ident[:])
         nc.sync.dma_start(list_b[:], offs3)
-        load_scales(nc.scalar, xt_s, xt_scales, range(3))
-        load_scales(nc.sync, xt_s, xt_scales, [3])
+        load_scales_repeated(nc.scalar, xt_s, xt_scales, range(3))
+        load_scales_repeated(nc.sync, xt_s, xt_scales, [3])
         nc.sync.dma_start(list_a[:], offs)
         nc.sync.dma_start(out=xt_w[:], in_=xt_words[0].rearrange("p c r -> p (c r)").bitcast(I32))
-        nc.sync.dma_start(out=tf_part0[:], in_=tf_dealt[:, 0:2, :])
-        load_live_rows(wb_s, wb_scales)
+        nc.sync.dma_start(out=tf_01[:], in_=tf_by_t[:, 0:2, :])
+        load_scales_over_zeros(wb_s, wb_scales)
         nc.sync.dma_start(list_f[:], offs2)
-        nc.sync.dma_start(out=ob_rows[:], in_=ob_dealt)
-        load_live_rows(wa_s, wa_scales)
-        nc.sync.dma_start(out=tf_part1[:], in_=tf_dealt[:, 2:3, :])
-        nc.sync.dma_start(out=tf_part2[:], in_=tf_dealt[:, 3:4, :])
+        nc.sync.dma_start(out=ob_rows[:], in_=ob_by_t)
+        load_scales_over_zeros(wa_s, wa_scales)
+        nc.sync.dma_start(out=tf_2[:], in_=tf_by_t[:, 2:3, :])
+        nc.sync.dma_start(out=tf_3[:], in_=tf_by_t[:, 3:4, :])
         nc.sync.dma_start(out=bi_pairs[:], in_=bi.rearrange("o (p m) -> p (o m)", m=2))
 
         xa_s = tile([P, J], U8, "xa_s")
         xb_w = tile([P, I], U32, "xb_w")
         xb_s = tile([P, I], U8, "xb_s")
-
-        def deal(copy, dst, src, run):
-            copy(
-                out=dst.rearrange("p (t c i) -> p c t i", t=PACK, i=run),
-                in_=src.rearrange("p (c i t) -> p c t i", t=PACK, i=run),
-            )
-
-        def deal_part(copy, dst, src, run, t0, t1):
-            copy(
-                out=dst.rearrange("p (t c i) -> p c t i", t=PACK, i=run)[:, :, t0:t1, :],
-                in_=src.rearrange("p (c i t) -> p c t i", t=PACK, i=run)[:, :, t0:t1, :],
-            )
-
         wa_sd = tile([P, R], U8, "wa_sd")
         wb_wd = tile([P, 2 * R], U8, "wb_wd")
         wb_sd = tile([P, R], U8, "wb_sd")
 
+        def deal(copy, dst, src, item_bytes, t_first=0, t_last=PACK):
+            run = LINE // item_bytes
+            copy(
+                out=dst.rearrange("p (t c i) -> p c t i", t=PACK, i=run)[:, :, t_first:t_last, :],
+                in_=src.rearrange("p (c i t) -> p c t i", t=PACK, i=run)[:, :, t_first:t_last, :],
+            )
+
         def pick_tf(t, first, last):
-            window = tf_rows[t].indirect(list_f[:, first // 16 : last // 16])
+            window = tf_rows[t].indirect(list_f[:, first // GROUP : last // GROUP])
             nc.scalar.activation(out=tf_picked[:, t, first:last], in_=window, func=COPY)
 
         def pick_words(dst, picks):
@@ -119,15 +118,16 @@ def tile_list_meet_timestable_added_bundlemax_kernel(
         pick_scales(xb_s, list_b)
         pick_scales(xa_s, list_a)
         pick_words(xb_w, list_b)
-        xa_w = tile([P, J], U32, "xa_w")
+        deal(nc.scalar.copy, wb_wd[:].bitcast(U16), wb_w[:].bitcast(U16), 2)
+        deal(nc.vector.tensor_copy, wb_sd[:], wb_s[:], 1)
+        xa_w = tile([P, J], U32, "xa_w", tag="wb_s")
         pick_words(xa_w, list_a)
-        deal(nc.scalar.copy, wb_wd[:].bitcast(U16), wb_w[:].bitcast(U16), 8)
-        deal(nc.vector.tensor_copy, wb_sd[:], wb_s[:], 16)
-        wa_wd = tile([P, R], U32, "wa_wd", tag="wb_s")
+        wa_wd = tile([P, R], U32, "wa_wd", tag="xt_w")
         deal(nc.vector.tensor_copy, wa_wd[:], wa_w[:].bitcast(U32), 4)
-        for t in range(3):
+        for t in range(PACK - 1):
             pick_tf(t, 0, J)
-        deal(nc.gpsimd.tensor_copy, wa_sd[:], wa_s[:], 16)
+        deal(nc.gpsimd.tensor_copy, wa_sd[:], wa_s[:], 1, 0, 2)
+        deal(nc.gpsimd.tensor_copy, wa_sd[:], wa_s[:], 1, 2, 4)
         pick_tf(3, 0, HALF)
         pick_tf(3, HALF, J)
 
@@ -165,26 +165,19 @@ def tile_list_meet_timestable_added_bundlemax_kernel(
                 op=op,
             )
 
-        def quantise(name, woven, width, fmt):
-            words = tile([P, width], U32, name + "_w")
-            scales = tile([P, width], U8, name + "_s")
-            nc.vector.quantize_mx(out=words[:].bitcast(fmt), scales=scales[:], in_=woven)
-            return words, scales
-
         zb = [
             first_stage("zb%d" % h, lambda t: wb_wd[:, 2 * t * P : 2 * (t + 1) * P].bitcast(E2M1), wb_sd, xb_w, xb_s, h)
             for h in range(2)
         ]
         hb = tile([P, I * PACK], BF16, "hb")
+        hb_halves = [hb[:, h * HALF * PACK : (h + 1) * HALF * PACK] for h in range(2)]
         for h in range(2):
-            combine(hb[:, h * HALF * PACK : (h + 1) * HALF * PACK], zb[h], ob_rows[:, :, h * HALF : (h + 1) * HALF], ALU.max)
+            combine(hb_halves[h], zb[h], ob_rows[:, :, h * HALF : (h + 1) * HALF], ALU.max)
         hb_w = tile([P, I], U32, "hb_w")
         hb_s = tile([P, I], U8, "hb_s")
         for h in range(2):
             cols = slice(h * HALF, (h + 1) * HALF)
-            nc.vector.quantize_mx(
-                out=hb_w[:, cols].bitcast(E4M3), scales=hb_s[:, cols], in_=hb[:, h * HALF * PACK : (h + 1) * HALF * PACK]
-            )
+            nc.vector.quantize_mx(out=hb_w[:, cols].bitcast(E4M3), scales=hb_s[:, cols], in_=hb_halves[h])
 
         za = [
             first_stage("za%d" % h, lambda t: wa_wd[:, t * P : (t + 1) * P].bitcast(E4M3), wa_sd, xa_w, xa_s, h)
@@ -194,7 +187,9 @@ def tile_list_meet_timestable_added_bundlemax_kernel(
         for h in range(2):
             ha = tile([P, HALF * PACK], BF16, "ha%d" % h)
             combine(ha[:], za[h], tf_picked[:, :, h * HALF : (h + 1) * HALF], ALU.mult)
-            ha_w, ha_s = quantise("haq%d" % h, ha[:], HALF, E5M2)
+            ha_w = tile([P, HALF], U32, "ha_w%d" % h)
+            ha_s = tile([P, HALF], U8, "ha_s%d" % h)
+            nc.vector.quantize_mx(out=ha_w[:].bitcast(E5M2), scales=ha_s[:], in_=ha[:])
             acc = ps.tile([P, I], F32, name="acc%d" % h)
             nc.tensor.matmul_mx(
                 out=acc[:],
@@ -215,4 +210,4 @@ def tile_list_meet_timestable_added_bundlemax_kernel(
                 axis=mybir.AxisListType.X,
                 op=ALU.max,
             )
-        nc.sync.dma_start(out=out.rearrange("(j p) s -> p j s", p=P), in_=best[:])
+            nc.sync.dma_start(out=out[h * HALF : (h + 1) * HALF, :], in_=best[:, h, :])

from contextlib import ExitStack

import concourse.mybir as mybir
from concourse.masks import make_identity

F32 = mybir.dt.float32
BF16 = mybir.dt.bfloat16
I32 = mybir.dt.int32
U32 = mybir.dt.uint32
U16 = mybir.dt.uint16
U8 = mybir.dt.uint8
E4M3 = mybir.dt.float8_e4m3fn_x4
E5M2 = mybir.dt.float8_e5m2_x4
E2M1 = mybir.dt.float4_e2m1fn_x4
ALU = mybir.AluOpType
COPY = mybir.ActivationFunctionType.Copy

K, T, J, I, R, C, S = 512, 512, 256, 256, 512, 512, 32
P = 128
PACK = 4
HALF = 128
GROUP = 16
QUADRANT = 32
LINE = 16
OUT_SCALE = 0.04
FLOPS = 2 * K * R * J + 2 * K * R * I + 2 * R * J * I


def tile_list_meet_timestable_added_bundlemax_kernel(
    tc, xt_words, xt_scales, wa_words, wa_scales, tf, wb_words, wb_scales, ob, bi, offs, offs2, offs3, out
):
    nc = tc.nc
    with ExitStack() as ctx:
        sb = ctx.enter_context(tc.tile_pool(name="sb", bufs=1))
        ps = ctx.enter_context(tc.psum_pool(name="ps", bufs=1))

        def tile(shape, dtype, name, tag=None):
            return sb.tile(shape, dtype, name=name, tag=tag or name, align_bytes=64)

        def load_scales_repeated(queue, dst, rows, quadrants):
            src = rows[0].bitcast(I32)
            for q in quadrants:
                queue.dma_start(
                    out=dst[QUADRANT * q : QUADRANT * (q + 1), :].bitcast(I32),
                    in_=src[4 * q : 4 * q + 4, :].unsqueeze(0).to_broadcast([QUADRANT // 4, 4, T // 4]),
                )

        def load_scales_over_zeros(dst, rows):
            nc.vector.memset(dst[:].bitcast(I32), 0)
            src = rows[0].bitcast(I32)
            for q in range(4):
                nc.sync.dma_start(
                    out=dst[QUADRANT * q : QUADRANT * q + 4, :].bitcast(I32), in_=src[4 * q : 4 * q + 4, :]
                )

        list_a = tile([P, J // GROUP], U16, "list_a")
        list_f = tile([P, J // GROUP], U16, "list_f")
        list_b = tile([P, I // GROUP], U16, "list_b")
        xt_w = tile([P, T], I32, "xt_w")
        xt_s = tile([P, T], U8, "xt_s")
        wa_w = tile([P, R], I32, "wa_w")
        wa_s = tile([P, R], U8, "wa_s")
        wb_w = tile([P, 2 * R], U8, "wb_w")
        wb_s = tile([P, R], U8, "wb_s")
        tf_01 = tile([P, 2, C], F32, "tf_01")
        tf_2 = tile([P, 1, C], F32, "tf_2")
        tf_3 = tile([P, 1, C], F32, "tf_3")
        tf_rows = [tf_01[:, 0, :], tf_01[:, 1, :], tf_2[:, 0, :], tf_3[:, 0, :]]
        ob_rows = tile([P, PACK, I], F32, "ob_rows")
        tf_picked = tile([P, PACK, J], F32, "tf_picked")
        bi_pairs = tile([P, 2], F32, "bi_pairs")
        ident = tile([P, P], F32, "ident")

        tf_by_t = tf.rearrange("(p t) c -> p t c", t=PACK)
        ob_by_t = ob.rearrange("(p t) i -> p t i", t=PACK)

        nc.gpsimd.dma_start(out=wb_w[:].bitcast(I32), in_=wb_words[0].bitcast(I32))
        nc.gpsimd.dma_start(out=wa_w[:], in_=wa_words[0].rearrange("p c r -> p (c r)").bitcast(I32))
        make_identity(nc, ident[:])
        nc.sync.dma_start(list_b[:], offs3)
        load_scales_repeated(nc.scalar, xt_s, xt_scales, range(3))
        load_scales_repeated(nc.sync, xt_s, xt_scales, [3])
        nc.sync.dma_start(list_a[:], offs)
        nc.sync.dma_start(out=xt_w[:], in_=xt_words[0].rearrange("p c r -> p (c r)").bitcast(I32))
        nc.sync.dma_start(out=tf_01[:], in_=tf_by_t[:, 0:2, :])
        load_scales_over_zeros(wb_s, wb_scales)
        nc.sync.dma_start(list_f[:], offs2)
        nc.sync.dma_start(out=ob_rows[:], in_=ob_by_t)
        load_scales_over_zeros(wa_s, wa_scales)
        nc.sync.dma_start(out=tf_2[:], in_=tf_by_t[:, 2:3, :])
        nc.sync.dma_start(out=tf_3[:], in_=tf_by_t[:, 3:4, :])
        nc.sync.dma_start(out=bi_pairs[:], in_=bi.rearrange("o (p m) -> p (o m)", m=2))

        xa_s = tile([P, J], U8, "xa_s")
        xb_w = tile([P, I], U32, "xb_w")
        xb_s = tile([P, I], U8, "xb_s")
        wa_sd = tile([P, R], U8, "wa_sd")
        wb_wd = tile([P, 2 * R], U8, "wb_wd")
        wb_sd = tile([P, R], U8, "wb_sd")

        def deal(copy, dst, src, item_bytes, t_first=0, t_last=PACK):
            run = LINE // item_bytes
            copy(
                out=dst.rearrange("p (t c i) -> p c t i", t=PACK, i=run)[:, :, t_first:t_last, :],
                in_=src.rearrange("p (c i t) -> p c t i", t=PACK, i=run)[:, :, t_first:t_last, :],
            )

        def pick_tf(t, first, last):
            window = tf_rows[t].indirect(list_f[:, first // GROUP : last // GROUP])
            nc.scalar.activation(out=tf_picked[:, t, first:last], in_=window, func=COPY)

        def pick_words(dst, picks):
            nc.vector.tensor_copy(out=dst[:], in_=xt_w[:].bitcast(U32).indirect(picks[:]))

        def pick_scales(dst, picks):
            nc.vector.tensor_copy(out=dst[:], in_=xt_s[:].indirect(picks[:]))

        pick_scales(xb_s, list_b)
        pick_scales(xa_s, list_a)
        pick_words(xb_w, list_b)
        deal(nc.scalar.copy, wb_wd[:].bitcast(U16), wb_w[:].bitcast(U16), 2)
        deal(nc.vector.tensor_copy, wb_sd[:], wb_s[:], 1)
        xa_w = tile([P, J], U32, "xa_w", tag="wb_s")
        pick_words(xa_w, list_a)
        wa_wd = tile([P, R], U32, "wa_wd", tag="xt_w")
        deal(nc.vector.tensor_copy, wa_wd[:], wa_w[:].bitcast(U32), 4)
        for t in range(PACK - 1):
            pick_tf(t, 0, J)
        deal(nc.gpsimd.tensor_copy, wa_sd[:], wa_s[:], 1, 0, 2)
        deal(nc.gpsimd.tensor_copy, wa_sd[:], wa_s[:], 1, 2, 4)
        pick_tf(3, 0, HALF)
        pick_tf(3, HALF, J)

        bi_ps = ps.tile([P, 2, P], F32, name="bi_ps")
        for m in range(2):
            nc.tensor.transpose(bi_ps[:, m, :], bi_pairs[:, m : m + 1].to_broadcast([P, P]), ident[:])
        bias = tile([P, I], F32, "bias")
        nc.scalar.activation(
            out=bias[:].rearrange("p (n m) -> p n m", m=2),
            in_=bi_ps[:].rearrange("p m n -> p n m"),
            func=COPY,
            scale=OUT_SCALE,
        )

        def first_stage(name, weights, weight_scales, x_w, x_s, h):
            z = ps.tile([P, PACK, HALF], F32, name=name)
            cols = slice(h * HALF, (h + 1) * HALF)
            for t in range(PACK):
                nc.tensor.matmul_mx(
                    out=z[:, t, :],
                    lhsT=weights(t),
                    lhsT_scale=weight_scales[:, t * P : (t + 1) * P],
                    rhs=x_w[:, cols].bitcast(E5M2),
                    rhs_scale=x_s[:, cols],
                    start=True,
                    stop=True,
                )
            return z

        def combine(woven, z, other, op):
            nc.vector.tensor_tensor(
                out=woven.rearrange("p (c i t) -> p c t i", t=PACK, i=2),
                in0=z[:].rearrange("p t (c i) -> p c t i", i=2),
                in1=other.rearrange("p t (c i) -> p c t i", i=2),
                op=op,
            )

        zb = [
            first_stage("zb%d" % h, lambda t: wb_wd[:, 2 * t * P : 2 * (t + 1) * P].bitcast(E2M1), wb_sd, xb_w, xb_s, h)
            for h in range(2)
        ]
        hb = tile([P, I * PACK], BF16, "hb")
        hb_halves = [hb[:, h * HALF * PACK : (h + 1) * HALF * PACK] for h in range(2)]
        for h in range(2):
            combine(hb_halves[h], zb[h], ob_rows[:, :, h * HALF : (h + 1) * HALF], ALU.max)
        hb_w = tile([P, I], U32, "hb_w")
        hb_s = tile([P, I], U8, "hb_s")
        for h in range(2):
            cols = slice(h * HALF, (h + 1) * HALF)
            nc.vector.quantize_mx(out=hb_w[:, cols].bitcast(E4M3), scales=hb_s[:, cols], in_=hb_halves[h])

        za = [
            first_stage("za%d" % h, lambda t: wa_wd[:, t * P : (t + 1) * P].bitcast(E4M3), wa_sd, xa_w, xa_s, h)
            for h in range(2)
        ]
        best = tile([P, 2, S], F32, "best")
        for h in range(2):
            ha = tile([P, HALF * PACK], BF16, "ha%d" % h)
            combine(ha[:], za[h], tf_picked[:, :, h * HALF : (h + 1) * HALF], ALU.mult)
            ha_w = tile([P, HALF], U32, "ha_w%d" % h)
            ha_s = tile([P, HALF], U8, "ha_s%d" % h)
            nc.vector.quantize_mx(out=ha_w[:].bitcast(E5M2), scales=ha_s[:], in_=ha[:])
            acc = ps.tile([P, I], F32, name="acc%d" % h)
            nc.tensor.matmul_mx(
                out=acc[:],
                lhsT=ha_w[:].bitcast(E5M2),
                lhsT_scale=ha_s[:],
                rhs=hb_w[:].bitcast(E4M3),
                rhs_scale=hb_s[:],
                start=True,
                stop=True,
            )
            scores = tile([P, I], F32, "scores%d" % h)
            nc.vector.scalar_tensor_tensor(
                out=scores[:], in0=acc[:], scalar=OUT_SCALE, in1=bias[:], op0=ALU.mult, op1=ALU.add
            )
            nc.vector.tensor_reduce(
                out=best[:, h, :],
                in_=scores[:].rearrange("p (s e) -> p s e", e=I // S),
                axis=mybir.AxisListType.X,
                op=ALU.max,
            )
            nc.sync.dma_start(out=out[h * HALF : (h + 1) * HALF, :], in_=best[:, h, :])
